import numpy as np
import ml_dtypes


def mxq(x, axis, fmt="e4m3"):
    dtype, down = {"e4m3": (ml_dtypes.float8_e4m3fn, 7), "e5m2": (ml_dtypes.float8_e5m2, 14)}[fmt]
    v = np.moveaxis(np.asarray(x, np.float32).astype(ml_dtypes.bfloat16).astype(np.float64), axis, -1)
    blocks = v.reshape(v.shape[:-1] + (-1, 32))
    amax = np.abs(blocks).max(-1, keepdims=True)
    byte = np.maximum(np.where(amax > 0, np.frexp(amax)[1] - 1 + 127, 0) - down, 1)
    scale = np.exp2(byte - 127.0)
    codes = (blocks / scale).astype(np.float32).astype(dtype).astype(np.float64)
    return np.moveaxis((codes * scale).reshape(v.shape), -1, axis)


WIDE = False


def mx_kscale(k):
    if not WIDE:
        return np.ones(k)
    levels = np.array([10, -10, 5, -5, 0])
    if k % 512:
        return np.exp2(np.random.permutation(np.resize(levels, k // 32))).repeat(32)
    a = np.empty((k // 512, 16))
    for p in range(k // 512):
        a[p, :8] = np.random.permutation(np.resize(levels, 8))
        for g in range(8):
            far = levels[np.abs(levels - a[p, g]) >= 10]
            a[p, g + 8] = far[np.random.randint(len(far))]
    return np.exp2(a.ravel()).repeat(32)


BF16 = ml_dtypes.bfloat16


def bf(x):
    return np.asarray(x, np.float32).astype(BF16)


def f64(x):
    return np.asarray(x).astype(np.float64)

E4M3FN = np.array([(-1.0 if i & 128 else 1.0) * ((1.0 + (i & 7) / 8.0) * 2.0 ** (((i >> 3) & 15) - 7) if i & 120 else (i & 7) * 2.0 ** -9) for i in range(256)])


def e4m3fn_bytes(y):
    return np.clip(np.asarray(y, np.float64), -448.0, 448.0).astype(np.float32).astype(ml_dtypes.float8_e4m3fn).view(np.uint8)


def e4m3fn_values(b):
    return E4M3FN[b]


T, E, D, N, B = 1024, 1024, 2048, 1536, 128


def setup_inputs():
    s, u = mx_kscale(E), mx_kscale(D)
    e = np.random.standard_normal((T, E)) * s
    f = np.random.standard_normal((T, D)) * u
    w = np.random.standard_normal((E + D, N)) / np.sqrt(E + D) / np.concatenate([s, u])[:, None]
    f_scale = (np.abs(f).reshape(T, D // B, B).max(axis=2) / 448.0).astype(np.float32)
    f_bytes = e4m3fn_bytes(f / np.repeat(f64(f_scale), B, axis=1))
    w_scale = (np.abs(w).reshape((E + D) // B, B, N // B, B).max(axis=(1, 3)) / 448.0).astype(np.float32)
    w_bytes = e4m3fn_bytes(w / np.repeat(np.repeat(f64(w_scale), B, axis=0), B, axis=1))
    return {"e": bf(e),
            "f_bytes": f_bytes,
            "f_scale": f_scale,
            "w_bytes": w_bytes,
            "w_scale": w_scale,
            "trust": bf(np.random.uniform(0.5, 1.5, (T, 1))),
            "b": bf(0.3 * np.random.standard_normal(N))}


def reference(e, f_bytes, f_scale, w_bytes, w_scale, trust, b):
    f = e4m3fn_values(f_bytes) * np.repeat(f64(f_scale), B, axis=1)
    w = e4m3fn_values(w_bytes) * np.repeat(np.repeat(f64(w_scale), B, axis=0), B, axis=1)
    wq = mxq(w, 0, "e4m3")
    a = mxq(f64(e), 1, "e4m3") @ wq[:E]
    c = mxq(f, 1, "e4m3") @ wq[E:]
    z = a + f64(trust) * c + f64(b)
    return z / (1.0 + np.exp(-z))

from contextlib import ExitStack

import concourse.mybir as mybir
from concourse.masks import make_identity

T, E, D, N = 1024, 1024, 2048, 1536
P = 128
K_PASS = 512
FLOPS = 2 * T * (E + D) * N

F32 = mybir.dt.float32
BF16 = mybir.dt.bfloat16
U32 = mybir.dt.uint32
U8 = mybir.dt.uint8
FP8 = mybir.dt.float8_e4m3fn
FP8X4 = mybir.dt.float8_e4m3fn_x4
ADD = mybir.AluOpType.add
MULT = mybir.AluOpType.mult
ACT = mybir.ActivationFunctionType

M_TILES = T // P
E_PASSES = E // K_PASS
F_PASSES = D // K_PASS
PASSES = E_PASSES + F_PASSES
F_BLOCKS = D // P

CHUNKS = [(0, 512), (512, 512), (1024, 256), (1280, 256)]
UNIT = 2048
F_ON_SCALAR = 16


def tile_drafter_feature_fusion_d2_kernel(tc, e, f_bytes, f_scale, w_bytes, w_scale, trust, b, out):
    nc = tc.nc
    with ExitStack() as ctx:
        once = ctx.enter_context(tc.tile_pool(name="once", bufs=1))
        codes8 = ctx.enter_context(tc.tile_pool(name="keep", bufs=1))
        work = ctx.enter_context(tc.tile_pool(name="work", bufs=3))
        psum = ctx.enter_context(tc.psum_pool(name="psum", bufs=2))

        e_v = e.rearrange("(p m) k -> p m k", m=M_TILES)
        f_v = f_bytes.rearrange("(p m) k -> p m k", m=M_TILES)
        o_v = out.rearrange("(p m) n -> p m n", m=M_TILES)
        w_v = w_bytes.rearrange("(g p t) n -> p g t n", p=P, t=4)

        wall = once.tile([P, 24 * 12], F32)
        nc.scalar.dma_start(out=wall[:], in_=w_scale.rearrange("r j -> (r j)").partition_broadcast(P))
        fs = once.tile([P, M_TILES * F_BLOCKS], F32)
        nc.scalar.dma_start(out=fs[:], in_=f_scale.rearrange("(p m) j -> p (m j)", m=M_TILES))

        zero = once.tile([P, 1], F32)
        nc.vector.memset(zero[:], 0.0)
        warm = once.tile([P, 1], F32)
        nc.scalar.activation(out=warm[:], in_=zero[:], func=ACT.Silu)

        units = []
        for c in range(len(CHUNKS)):
            width = CHUNKS[c][1]
            per = UNIT // (4 * width)
            for g in range(0, PASSES, per):
                units.append((c, g, per))

        wb = {}
        eb = {}
        fb = {}

        def load_w(c, g, per):
            n0, width = CHUNKS[c]
            t = once.tile([P, UNIT], U8, name="wb%d_%d" % (c, g))
            if per == 1:
                nc.sync.dma_start(out=t[:].rearrange("p (t n) -> p t n", t=4), in_=w_v[:, g, :, n0:n0 + width])
            else:
                for i in range(per):
                    part = UNIT // per
                    nc.sync.dma_start(
                        out=t[:, i * part:(i + 1) * part].rearrange("p (t n) -> p t n", t=4),
                        in_=w_v[:, g + i, :, n0:n0 + width])
            wb[(c, g)] = t

        def load_x(m):
            t = once.tile([P, E], BF16, name="eb%d" % m)
            nc.sync.dma_start(out=t[:], in_=e_v[:, m, :])
            eb[m] = t
            t2 = once.tile([P, D], U8, name="fb%d" % m)
            nc.sync.dma_start(out=t2[:], in_=f_v[:, m, :])
            fb[m] = t2

        c0 = [u for u in units if u[0] == 0]
        rest = [u for u in units if u[0] != 0]
        load_w(*c0[0])
        load_x(0)
        for u in c0[1:]:
            load_w(*u)
        load_x(1)
        load_x(2)
        tr = once.tile([P, M_TILES], BF16)
        nc.sync.dma_start(out=tr[:], in_=trust.rearrange("(p m) o -> p (m o)", m=M_TILES))
        bt = once.tile([P, N], BF16)
        nc.sync.dma_start(out=bt[:], in_=b.partition_broadcast(P))
        load_x(3)
        for i, u in enumerate(rest):
            load_w(*u)
            if i < 4:
                load_x(4 + i)

        ident = once.tile([P, P], F32)
        make_identity(nc, ident[:])

        ws = once.tile([P, PASSES, 12], F32)
        wall_v = wall[:].rearrange("p (g q j) -> p g q j", g=PASSES, q=4)
        for q in range(4):
            rows = slice(32 * q, 32 * q + 32)
            nc.gpsimd.tensor_copy(out=ws[rows, :, :], in_=wall_v[rows, :, q, :])

        wq = {}

        def prep_w(c, g, per):
            n0, width = CHUNKS[c]
            planes = work.tile([P, UNIT], BF16, name="planes")
            nc.scalar.copy(out=planes[:], in_=wb[(c, g)][:].bitcast(FP8))
            laced = work.tile([P, UNIT], BF16, align_bytes=64, name="laced")
            part = UNIT // per
            for i in range(per):
                src = planes[:, i * part:(i + 1) * part].rearrange("p (t c i) -> p c t i", t=4, i=4)
                dst = laced[:, i * part:(i + 1) * part].rearrange("p (c i t) -> p c t i", t=4, i=4)
                for j in range(width // P):
                    blk = slice(j * 32, (j + 1) * 32)
                    jj = n0 // P + j
                    nc.vector.tensor_scalar(out=dst[:, blk], in0=src[:, blk], scalar1=ws[:, g + i, jj:jj + 1],
                                            scalar2=None, op0=MULT)
            wc = once.tile([P, UNIT // 4], U32, align_bytes=64, name="wc%d_%d" % (c, g))
            wsc = once.tile([P, UNIT // 4], U8, align_bytes=64, name="wsc%d_%d" % (c, g))
            nc.vector.quantize_mx(out=wc[:].bitcast(FP8X4), scales=wsc[:], in_=laced[:])
            for i in range(per):
                cols = slice(i * width, (i + 1) * width)
                wq[(c, g + i)] = (wc, wsc, cols)

        xq = {}

        def turn(words, g0, name, gr, goff):
            bank = psum.tile([P, 2, 2, P], F32, name="turn")
            for h in range(2):
                for u in range(2):
                    s = 256 * (g0 + h) + u
                    nc.tensor.transpose(bank[:, h, u, :], words[:, s:256 * (g0 + h + 1):2], ident[:])
            dst = gr[:, goff:goff + 1024].bitcast(F32).rearrange("p (h r u) -> p h r u", h=2, u=2)
            nc.scalar.copy(out=dst, in_=bank[:].rearrange("p h u r -> p h r u"))

        def prep_x(m):
            ge = work.tile([P, E], BF16, align_bytes=64, name="ge")
            turn(eb[m][:].bitcast(F32), 0, "e", ge, 0)
            ec = once.tile([P, E // 4], U32, align_bytes=64, name="ec%d" % m)
            es = once.tile([P, E // 4], U8, align_bytes=64, name="es%d" % m)
            nc.vector.quantize_mx(out=ec[:].bitcast(FP8X4), scales=es[:], in_=ge[:])
            fw = work.tile([P, D], BF16, name="fw")
            for j in range(F_BLOCKS):
                cols = slice(j * P, (j + 1) * P)
                sc = fs[:, m * F_BLOCKS + j:m * F_BLOCKS + j + 1]
                if j < F_ON_SCALAR:
                    nc.scalar.activation(out=fw[:, cols], in_=fb[m][:, cols].bitcast(FP8), func=ACT.Copy, scale=sc)
                else:
                    nc.vector.tensor_scalar(out=fw[:, cols], in0=fb[m][:, cols].bitcast(FP8), scalar1=sc,
                                            scalar2=None, op0=MULT)
            gf = work.tile([P, D], BF16, align_bytes=64, name="gf")
            turn(fw[:].bitcast(F32), 0, "f", gf, 0)
            turn(fw[:].bitcast(F32), 2, "f", gf, 1024)
            fc = once.tile([P, D // 4], U32, align_bytes=64, name="fc%d" % m)
            fsc = once.tile([P, D // 4], U8, align_bytes=64, name="fsc%d" % m)
            nc.vector.quantize_mx(out=fc[:].bitcast(FP8X4), scales=fsc[:], in_=gf[:])
            for g in range(E_PASSES):
                xq[(m, g)] = (ec, es, slice(g * P, (g + 1) * P))
            for g in range(F_PASSES):
                xq[(m, E_PASSES + g)] = (fc, fsc, slice(g * P, (g + 1) * P))

        def mm(acc, m, c, passes):
            for g in passes:
                xc, xs, xcols = xq[(m, g)]
                wc, wsc, wcols = wq[(c, g)]
                nc.tensor.matmul_mx(out=acc, lhsT=xc[:, xcols].bitcast(FP8X4), lhsT_scale=xs[:, xcols],
                                    rhs=wc[:, wcols].bitcast(FP8X4), rhs_scale=wsc[:, wcols],
                                    start=(g == passes[0]), stop=(g == passes[-1]))

        def product(m, c):
            n0, width = CHUNKS[c]
            acc_a = psum.tile([P, 512], F32, name="acc", bufs=6)
            a = acc_a[:, 0:width]
            if width == 512:
                acc_c = psum.tile([P, 512], F32, name="acc", bufs=6)
                cc = acc_c[:, 0:width]
            else:
                cc = acc_a[:, width:2 * width]
            mm(a, m, c, list(range(E_PASSES)))
            mm(cc, m, c, list(range(E_PASSES, PASSES)))
            t = work.tile([P, 512], F32, name="t")
            nc.vector.tensor_tensor(out=t[:, 0:width], in0=a, in1=bt[:, n0:n0 + width], op=ADD)
            z = work.tile([P, 512], F32, name="z")
            nc.vector.scalar_tensor_tensor(out=z[:, 0:width], in0=cc, scalar=tr[:, m:m + 1], in1=t[:, 0:width],
                                           op0=MULT, op1=ADD)
            o = work.tile([P, 512], F32, name="o", bufs=4)
            nc.scalar.activation(out=o[:, 0:width], in_=z[:, 0:width], func=ACT.Silu)
            nc.sync.dma_start(out=o_v[:, m, n0:n0 + width], in_=o[:, 0:width])

        prep_w(*c0[0])
        prep_x(0)
        for u in c0[1:]:
            prep_w(*u)
        prep_x(1)
        for m in range(M_TILES):
            product(m, 0)
            if m + 2 < M_TILES:
                prep_x(m + 2)
        for c in range(1, len(CHUNKS)):
            for u in units:
                if u[0] == c:
                    prep_w(*u)
            for m in range(M_TILES):
                product(m, c)
